import numpy as np
import ml_dtypes


def mxq(x, axis, fmt="e4m3"):
    dtype, down = {"e4m3": (ml_dtypes.float8_e4m3fn, 7), "e5m2": (ml_dtypes.float8_e5m2, 14)}[fmt]
    v = np.moveaxis(np.asarray(x, np.float32).astype(ml_dtypes.bfloat16).astype(np.float64), axis, -1)
    blocks = v.reshape(v.shape[:-1] + (-1, 32))
    amax = np.abs(blocks).max(-1, keepdims=True)
    byte = np.maximum(np.where(amax > 0, np.frexp(amax)[1] - 1 + 127, 0) - down, 1)
    scale = np.exp2(byte - 127.0)
    codes = (blocks / scale).astype(np.float32).astype(dtype).astype(np.float64)
    return np.moveaxis((codes * scale).reshape(v.shape), -1, axis)


WIDE = False


def mx_kscale(k):
    if not WIDE:
        return np.ones(k)
    levels = np.array([10, -10, 5, -5, 0])
    if k % 512:
        return np.exp2(np.random.permutation(np.resize(levels, k // 32))).repeat(32)
    a = np.empty((k // 512, 16))
    for p in range(k // 512):
        a[p, :8] = np.random.permutation(np.resize(levels, 8))
        for g in range(8):
            far = levels[np.abs(levels - a[p, g]) >= 10]
            a[p, g + 8] = far[np.random.randint(len(far))]
    return np.exp2(a.ravel()).repeat(32)


def f64(x):
    return np.asarray(x).astype(np.float64)


def striped(idx):
    return np.tile(idx.reshape(-1, 16).T, (8, 1)).astype(np.uint16)


def unstriped(offs):
    return offs[:16].T.reshape(-1).astype(np.int64)


def pack_weight(w):
    k, n = w.shape
    w = f64(np.asarray(w, np.float32).astype(ml_dtypes.bfloat16)).reshape(k // 32, 32, n)
    amax = np.abs(w).max(1)
    byte = np.clip(np.where(amax > 0, np.frexp(amax)[1] - 1 + 127 - 7, 1), 1, 254)
    scaled = (w * np.exp2(127.0 - byte)[:, None, :]).reshape(k, n).astype(np.float32)
    words = np.ascontiguousarray(scaled.reshape(k // 512, 128, 4, n).transpose(0, 1, 3, 2)).astype(ml_dtypes.float8_e4m3fn).view(np.uint8)
    return words, np.ascontiguousarray(byte.astype(np.uint8).reshape(k // 512, 16, n))


def unpack_weight(words, scales):
    g, p, n, _ = words.shape
    vals = np.ascontiguousarray(words).view(ml_dtypes.float8_e4m3fn).astype(np.float64) * np.repeat(np.exp2(scales.astype(np.float64) - 127.0), 8, axis=1)[..., None]
    return vals.transpose(0, 1, 3, 2).reshape(g * 512, n)


def gelu(v):
    return 0.5 * v * (1.0 + np.tanh(np.sqrt(2.0 / np.pi) * (v + 0.044715 * v**3)))


K, T, E, C, N = 512, 512, 12, 128, 512
TOP = 3
M = 1024


def by_expert(wq, xq):
    return np.concatenate([wq[e].T @ xq[:, e * C:(e + 1) * C] for e in range(E)], axis=1)


def setup_inputs():
    n = np.random.standard_normal
    s = mx_kscale(K)[:, None]
    deal = np.repeat(np.arange(E), C).reshape(TOP, T)[:, np.random.permutation(T)]
    deal = np.take_along_axis(deal, np.argsort(np.random.rand(TOP, T), axis=0), axis=0)
    for _ in range(8):
        s_, t_ = np.random.permutation(T).reshape(2, -1); r = np.random.randint(TOP, size=T // 2); x, y = deal[r, s_].copy(), deal[r, t_].copy()
        ok = ~((deal[:, s_] == y).any(0) | (deal[:, t_] == x).any(0)); deal[r[ok], s_[ok]] = y[ok]; deal[r[ok], t_[ok]] = x[ok]
    order = np.lexsort((np.random.rand(TOP * T), deal.reshape(-1)))
    slot_token = order % T; pos = np.empty(TOP * T, np.int64); pos[order] = np.arange(TOP * T); pos = pos.reshape(TOP, T)
    g = np.random.uniform(0.5, 1.5, (TOP, T)); g = g / g.sum(0)
    packed = [pack_weight(m) for m in n((E, K, N)) / np.sqrt(K) / s[None]]
    r = mx_kscale(M)[:, None]
    return {
        "uT": (n((M, T)) * r).astype(np.float32),
        "wu": (n((M, K)) / np.sqrt(M) / r * s.T).astype(np.float32),
        "w_words": np.stack([m[0] for m in packed]),
        "w_scales": np.stack([m[1] for m in packed]),
        "b": (0.3 * n((N, E))).astype(np.float32),
        "gate": np.stack([np.tile(r, (N, 1)) for r in g]).astype(np.float32),
        "offs": striped(slot_token),
        "pos1": striped(pos[0]),
        "pos2": striped(pos[1]),
        "pos3": striped(pos[2]),
    }


def reference(uT, wu, w_words, w_scales, b, gate, offs, pos1, pos2, pos3):
    idx = unstriped(offs)
    w = np.stack([unpack_weight(w_words[e], w_scales[e]) for e in range(E)])
    x = mxq(f64(wu), 0, "e4m3").T @ mxq(f64(uT), 0, "e4m3")
    xq = mxq(x[:, idx], 0, "e4m3")
    y = by_expert(w, xq)
    y = gelu(y + np.repeat(f64(b), C, axis=1))
    return sum(f64(gate[r]) * y[:, unstriped(p)] for r, p in enumerate((pos1, pos2, pos3)))

@@ -1,0 +1,323 @@
+from contextlib import ExitStack
+
+import concourse.mybir as mybir
+from concourse.masks import make_identity
+
+F, K, T, E, C, N = 1024, 512, 512, 12, 128, 512
+TOP = 3
+S = E * C
+FLOPS = 2 * F * K * T + 2 * K * N * S
+BYTES = 4 * F * T + 4 * F * K + E * K * N + E * 16 * N + 4 * N * E + 4 * TOP * T + 2 * 128 * (S + TOP * T) // 16 + 4 * N * T
+
+F32 = mybir.dt.float32
+BF16 = mybir.dt.bfloat16
+I32 = mybir.dt.int32
+U32 = mybir.dt.uint32
+U16 = mybir.dt.uint16
+U8 = mybir.dt.uint8
+FP8X4 = mybir.dt.float8_e4m3fn_x4
+MULT = mybir.AluOpType.mult
+ADD = mybir.AluOpType.add
+GELU = mybir.ActivationFunctionType.Gelu_apprx_tanh
+
+P = 128
+PACK = 4
+HALF = T // 2
+WINDOW = 704
+U_SPLIT = 320
+M_SPLIT = 80
+PIECES = ((0, 4), (4, 8), (8, 10), (10, 11), (11, 12))
+ORDER = "g0 g1 q0 g2 g3 q1 g4 q2 q3 q4"
+GATHER_TILES = (((0,), None), ((1,), None), ((2, 3), 0), ((4,), 1))
+LATER_BANKS = (0, 3, 2)
+W_LOADS = ((0, 4), (4, 8), (8, 12))
+
+
+def tile_moe_prv_lin_gelu_kernel(
+    tc, uT, wu, w_words, w_scales, b, gate, offs, pos1, pos2, pos3, out
+):
+    nc = tc.nc
+    with ExitStack() as ctx:
+        keep = ctx.enter_context(tc.tile_pool(name="keep", bufs=1))
+        ring = ctx.enter_context(tc.tile_pool(name="ring", bufs=2))
+        psum = ctx.enter_context(tc.psum_pool(name="psum", bufs=1))
+
+        def held(shape, dtype, name, tag=None):
+            return keep.tile(shape, dtype, name=name, tag=tag or name, align_bytes=64)
+
+        def bank(index):
+            return psum.tile([P, 512], F32, name="bank%d" % index, tag="bank%d" % index)
+
+        warm = held([P, 8], F32, "warm")
+        nc.vector.memset(warm[:], 0.0)
+        warm_out = held([P, 8], F32, "warm_out")
+        nc.scalar.activation(out=warm_out[:], in_=warm[:], func=GELU)
+
+        w_scale = held([P, E, N], U8, "w_scale")
+        nc.gpsimd.memset(w_scale[:].bitcast(I32), 0)
+        x_pairs = [held([P, WINDOW], U32, "x_pair%d" % h) for h in range(2)]
+        for x_pair in x_pairs:
+            nc.gpsimd.memset(x_pair[:, T:], 0)
+        ident = held([P, P], F32, "ident")
+        make_identity(nc, ident[:])
+
+        u_rows = uT.rearrange("(a p j) t -> a p j t", p=P, j=PACK)
+        wu_rows = wu.rearrange("(a p j) k -> a p j k", p=P, j=PACK)
+        u_raw = [held([P, PACK, T], F32, "u_raw%d" % a) for a in range(2)]
+        wu_raw0 = held([P, PACK, K], F32, "wu_raw0")
+        wu_raw1 = [held([P, 2, K], F32, "wu_raw1_%d" % h) for h in range(2)]
+        nc.sync.dma_start(out=u_raw[0][:], in_=u_rows[0])
+        nc.sync.dma_start(out=wu_raw0[:], in_=wu_rows[0])
+        nc.sync.dma_start(out=u_raw[1][:], in_=u_rows[1])
+        for h in range(2):
+            nc.sync.dma_start(out=wu_raw1[h][:], in_=wu_rows[1][:, 2 * h : 2 * h + 2, :])
+        slot_list = keep.tile([P, S // 16], U16, name="slot_list")
+        nc.sync.dma_start(slot_list[:], offs)
+        scale_rows = w_scales.rearrange("e a (q r) n -> r q (e a) n", r=4)
+        for r in range(4):
+            nc.sync.dma_start(out=w_scale[r:P:32, :, :].bitcast(I32), in_=scale_rows[r].bitcast(I32))
+        bias = [held([P, E], F32, "bias%d" % j) for j in range(N // P)]
+        w_code = {}
+        for number, (e0, e1) in enumerate(W_LOADS):
+            w_tile = held([P, e1 - e0, N], U32, "w_code%d" % e0)
+            nc.sync.dma_start(
+                out=w_tile[:].bitcast(I32),
+                in_=w_words[e0:e1, 0].rearrange("e p n r -> p e (n r)").bitcast(I32),
+            )
+            for e in range(e0, e1):
+                w_code[e] = w_tile[:, e - e0, :]
+            if number == 0:
+                nc.sync.dma_start(out=bias[0][:], in_=b[0:P, :])
+        for j in range(1, N // P):
+            nc.sync.dma_start(out=bias[j][:], in_=b[j * P : (j + 1) * P, :])
+        pos_lists = []
+        for r, pos in enumerate((pos1, pos2, pos3)):
+            pos_list = keep.tile([P, T // 16], U16, name="pos_list%d" % r)
+            nc.sync.dma_start(pos_list[:], pos)
+            pos_lists.append(pos_list)
+        gates = held([P, TOP, T], F32, "gates")
+        nc.sync.dma_start(out=gates[:], in_=gate[:, 0:P, :].rearrange("r p t -> p r t"))
+
+        u_code, u_scale = [], []
+
+        def quantise_u(a):
+            grouped = held([P, T, PACK], BF16, "u_grouped%d" % a)
+            dst = grouped[:].rearrange("p (c i) j -> p c j i", i=4)
+            src = u_raw[a][:].rearrange("p j (c i) -> p c j i", i=4)
+            nc.vector.tensor_copy(out=dst[:, : U_SPLIT // 4], in_=src[:, : U_SPLIT // 4])
+            nc.scalar.copy(out=dst[:, U_SPLIT // 4 :], in_=src[:, U_SPLIT // 4 :])
+            codes = held([P, T], U32, "u_code%d" % a)
+            scales = held([P, T], U8, "u_scale%d" % a)
+            nc.vector.quantize_mx(
+                out=codes[:].bitcast(FP8X4), scales=scales[:], in_=grouped[:].rearrange("p t j -> p (t j)")
+            )
+            u_code.append(codes)
+            u_scale.append(scales)
+
+        quantise_u(0)
+
+        wu_grouped0 = held([P, PACK, P, PACK], BF16, "wu_grouped0")
+        dst = wu_grouped0[:].rearrange("p t m j -> p m t j")
+        src = wu_raw0[:].rearrange("p j (m t) -> p m t j", t=PACK)
+        nc.vector.tensor_copy(out=dst[:, :M_SPLIT], in_=src[:, :M_SPLIT])
+        nc.scalar.copy(out=dst[:, M_SPLIT:], in_=src[:, M_SPLIT:])
+        wu_code0 = held([P, K], U32, "wu_code0")
+        wu_scale0 = held([P, K], U8, "wu_scale0")
+        nc.vector.quantize_mx(
+            out=wu_code0[:].bitcast(FP8X4), scales=wu_scale0[:], in_=wu_grouped0[:].rearrange("p t m j -> p (t m j)")
+        )
+
+        x_banks = {}
+        for t in range(PACK):
+            for h in range(2):
+                x_banks[t, h] = bank(4 * (t // 2) + 2 * h + t % 2)
+                nc.tensor.matmul_mx(
+                    out=x_banks[t, h][:, :HALF],
+                    lhsT=wu_code0[:, t * P : (t + 1) * P].bitcast(FP8X4),
+                    lhsT_scale=wu_scale0[:, t * P : (t + 1) * P],
+                    rhs=u_code[0][:, h * HALF : (h + 1) * HALF].bitcast(FP8X4),
+                    rhs_scale=u_scale[0][:, h * HALF : (h + 1) * HALF],
+                    start=True,
+                    stop=False,
+                )
+
+        quantise_u(1)
+
+        wu_grouped1 = [held([P, 2, P, PACK], BF16, "wu_grouped1_%d" % g) for g in range(2)]
+        for h in range(2):
+            src = wu_raw1[h][:].rearrange("p j (m t) -> p m t j", t=PACK)
+            for g in range(2):
+                dst = wu_grouped1[g][:].rearrange("p t m j -> p m t j")[:, :, :, 2 * h : 2 * h + 2]
+                if g == 0:
+                    nc.vector.tensor_copy(out=dst, in_=src[:, :, 0:2, :])
+                else:
+                    nc.scalar.copy(out=dst, in_=src[:, :, 2:4, :])
+        for g in range(2):
+            codes = held([P, 2 * P], U32, "wu_code1_%d" % g)
+            scales = held([P, 2 * P], U8, "wu_scale1_%d" % g)
+            nc.vector.quantize_mx(
+                out=codes[:].bitcast(FP8X4), scales=scales[:], in_=wu_grouped1[g][:].rearrange("p t m j -> p (t m j)")
+            )
+            pairs = x_pairs[g][:].bitcast(BF16).rearrange("p (w i) -> p w i", i=2)
+            for h in range(2):
+                for i in range(2):
+                    x_bank = x_banks[2 * g + i, h]
+                    nc.tensor.matmul_mx(
+                        out=x_bank[:, :HALF],
+                        lhsT=codes[:, i * P : (i + 1) * P].bitcast(FP8X4),
+                        lhsT_scale=scales[:, i * P : (i + 1) * P],
+                        rhs=u_code[1][:, h * HALF : (h + 1) * HALF].bitcast(FP8X4),
+                        rhs_scale=u_scale[1][:, h * HALF : (h + 1) * HALF],
+                        start=False,
+                        stop=True,
+                    )
+                    dst = pairs[:, h * HALF : (h + 1) * HALF, i]
+                    if g == 0 and h == 1:
+                        nc.vector.tensor_copy(out=dst, in_=x_bank[:, :HALF])
+                    else:
+                        nc.scalar.copy(out=dst, in_=x_bank[:, :HALF])
+
+        y = {0: held([P, S], F32, "y0")}
+        slot_code, slot_scale, woven, gathered = {}, {}, {}, {}
+
+        def gather_piece(piece):
+            e0, e1 = PIECES[piece]
+            width = (e1 - e0) * C
+            for members, after in GATHER_TILES:
+                if piece == members[0]:
+                    total = sum((PIECES[m][1] - PIECES[m][0]) * C for m in members)
+                    tile = held([P, 2 * total], U32, "gathered%d" % piece, None if after is None else "woven%d" % after)
+                    start = 0
+                    for m in members:
+                        size = 2 * (PIECES[m][1] - PIECES[m][0]) * C
+                        gathered[m] = tile[:, start : start + size].rearrange("p (g s) -> p g s", g=2)
+                        start = start + size
+            for g in range(2):
+                nc.vector.tensor_copy(
+                    out=gathered[piece][:, g, :], in_=x_pairs[g][:].indirect(slot_list[:, e0 * C // 16 : e1 * C // 16])
+                )
+            woven[piece] = held([P, width, 2], U32, "woven%d" % piece)
+            nc.scalar.copy(out=woven[piece][:], in_=gathered[piece].rearrange("p g s -> p s g"))
+
+        def quantise_piece(piece):
+            e0, e1 = PIECES[piece]
+            width = (e1 - e0) * C
+            slot_code[piece] = held([P, width], U32, "slot_code%d" % piece)
+            slot_scale[piece] = held([P, width], U8, "slot_scale%d" % piece)
+            nc.vector.quantize_mx(
+                out=slot_code[piece][:].bitcast(FP8X4),
+                scales=slot_scale[piece][:],
+                in_=woven[piece][:].rearrange("p s g -> p (s g)").bitcast(BF16),
+            )
+
+        piece_of = {e: piece for piece, (e0, e1) in enumerate(PIECES) for e in range(e0, e1)}
+
+        def products(e0, e1, j):
+            acc = bank(piece_of[e0] % 4 if j == 0 else LATER_BANKS[e0 // 4])
+            for e in range(e0, e1):
+                piece = piece_of[e]
+                slots = slice((e - PIECES[piece][0]) * C, (e - PIECES[piece][0] + 1) * C)
+                nc.tensor.matmul_mx(
+                    out=acc[:, (e - e0) * C : (e - e0 + 1) * C],
+                    lhsT=w_code[e][:, j * P : (j + 1) * P].bitcast(FP8X4),
+                    lhsT_scale=w_scale[:, e, j * P : (j + 1) * P],
+                    rhs=slot_code[piece][:, slots].bitcast(FP8X4),
+                    rhs_scale=slot_scale[piece][:, slots],
+                    start=True,
+                    stop=True,
+                )
+            return acc
+
+        def gelus(e0, e1, j, acc):
+            if j not in y:
+                y[j] = held([P, S], F32, "y%d" % j, "bias%d" % (j - 1))
+            for e in range(e0, e1):
+                nc.scalar.activation(
+                    out=y[j][:, e * C : (e + 1) * C],
+                    in_=acc[:, (e - e0) * C : (e - e0 + 1) * C],
+                    func=GELU,
+                    bias=bias[j][:, e : e + 1],
+                )
+
+        def experts(j):
+            for e0, e1 in W_LOADS:
+                gelus(e0, e1, j, products(e0, e1, j))
+
+        for step in ORDER.split():
+            piece = int(step[1:])
+            if step[0] == "g":
+                gather_piece(piece)
+            else:
+                quantise_piece(piece)
+                e0, e1 = PIECES[piece]
+                gelus(e0, e1, 0, products(e0, e1, 0))
+
+        def gated(j, r, cols, term):
+            nc.vector.tensor_tensor(
+                out=term[:, cols],
+                in0=y[j][:].indirect(pos_lists[r][:, cols.start // 16 : cols.stop // 16]),
+                in1=gates[:, r, cols],
+                op=MULT,
+            )
+
+        def gated_terms(j):
+            terms = []
+            for r in range(TOP):
+                term = ring.tile([P, T], F32, name="term%d" % r, tag="term%d" % r, align_bytes=64)
+                gated(j, r, slice(0, T), term)
+                terms.append(term)
+            return terms
+
+        def turned_sum(j, terms):
+            turned = bank(4 + j % 2)
+            for block in range(T // P):
+                cols = slice(block * P, (block + 1) * P)
+                for r in range(TOP):
+                    nc.tensor.matmul(
+                        out=turned[:, cols],
+                        lhsT=terms[r][:, cols],
+                        rhs=ident[:],
+                        is_transpose=True,
+                        start=(r == 0),
+                        stop=(r == TOP - 1),
+                    )
+            return turned
+
+        def turn_back_and_store(j, turned):
+            staged = ring.tile([P, T], F32, name="staged", tag="staged", align_bytes=64)
+            nc.scalar.copy(out=staged[:], in_=turned[:])
+            back = bank(6 + j % 2)
+            for block in range(T // P):
+                cols = slice(block * P, (block + 1) * P)
+                nc.tensor.transpose(back[:, cols], staged[:, cols], ident[:])
+            result = ring.tile([P, T], F32, name="result", tag="result", align_bytes=64)
+            nc.scalar.copy(out=result[:], in_=back[:])
+            nc.sync.dma_start(out=out[j * P : (j + 1) * P, :], in_=result[:])
+
+        experts(1)
+        terms = gated_terms(0)
+        experts(2)
+        turned = turned_sum(0, terms)
+        terms = gated_terms(1)
+        accs = [products(e0, e1, 3) for e0, e1 in W_LOADS]
+        turn_back_and_store(0, turned)
+        for (e0, e1), acc in zip(W_LOADS, accs):
+            gelus(e0, e1, 3, acc)
+        turned = turned_sum(1, terms)
+        terms = gated_terms(2)
+        turn_back_and_store(1, turned)
+        turn_back_and_store(2, turned_sum(2, terms))
+
+        last = N // P - 1
+        last_terms = [held([P, T], F32, "last_term%d" % r) for r in range(TOP)]
+        gated(last, 0, slice(0, T), last_terms[0])
+        gated(last, 1, slice(0, T), last_terms[1])
+        halves = [slice(0, HALF), slice(HALF, T)]
+        gated(last, 2, halves[0], last_terms[2])
+        partial = held([P, T], F32, "partial")
+        nc.vector.tensor_tensor(out=partial[:], in0=last_terms[0][:], in1=last_terms[1][:], op=ADD)
+        gated(last, 2, halves[1], last_terms[2])
+        for h, cols in enumerate(halves):
+            result = held([P, HALF], F32, "last_result%d" % h)
+            nc.vector.tensor_tensor(out=result[:], in0=partial[:, cols], in1=last_terms[2][:, cols], op=ADD)
+            nc.sync.dma_start(out=out[last * P : (last + 1) * P, cols], in_=result[:])

@@ -24,7 +24,9 @@ P = 128
 PACK = 4
 HALF = T // 2
 WINDOW = 704
-U_SPLIT = 320
+TOKEN_BLOCKS = ((0, 128), (128, 256), (256, 384), (384, 512))
+U_LOADS = tuple((a, t0, t1, 80 if a == 0 or t1 == T else 128) for t0, t1 in TOKEN_BLOCKS for a in range(2))
+X_BANKS = (0, 1, 2, 3, 4, 5, 6, 7)
 M_SPLIT = 80
 PIECES = ((0, 4), (4, 8), (8, 10), (10, 11), (11, 12))
 ORDER = "g0 g1 q0 g2 g3 q1 g4 q2 q3 q4"
@@ -63,14 +65,14 @@ def tile_moe_prv_lin_gelu_kernel(
 
         u_rows = uT.rearrange("(a p j) t -> a p j t", p=P, j=PACK)
         wu_rows = wu.rearrange("(a p j) k -> a p j k", p=P, j=PACK)
-        u_raw = [held([P, PACK, T], F32, "u_raw%d" % a) for a in range(2)]
-        wu_raw0 = held([P, PACK, K], F32, "wu_raw0")
-        wu_raw1 = [held([P, 2, K], F32, "wu_raw1_%d" % h) for h in range(2)]
-        nc.sync.dma_start(out=u_raw[0][:], in_=u_rows[0])
-        nc.sync.dma_start(out=wu_raw0[:], in_=wu_rows[0])
-        nc.sync.dma_start(out=u_raw[1][:], in_=u_rows[1])
-        for h in range(2):
-            nc.sync.dma_start(out=wu_raw1[h][:], in_=wu_rows[1][:, 2 * h : 2 * h + 2, :])
+        wu_raw = [held([P, PACK, K], F32, "wu_raw%d" % a) for a in range(2)]
+        for a in range(2):
+            nc.sync.dma_start(out=wu_raw[a][:], in_=wu_rows[a])
+        u_raw = []
+        for a, t0, t1, split in U_LOADS:
+            raw = held([P, PACK, t1 - t0], F32, "u_raw%d_%d" % (a, t0))
+            nc.sync.dma_start(out=raw[:], in_=u_rows[a][:, :, t0:t1])
+            u_raw.append(raw)
         slot_list = keep.tile([P, S // 16], U16, name="slot_list")
         nc.sync.dma_start(slot_list[:], offs)
         scale_rows = w_scales.rearrange("e a (q r) n -> r q (e a) n", r=4)
@@ -98,84 +100,85 @@ def tile_moe_prv_lin_gelu_kernel(
         gates = held([P, TOP, T], F32, "gates")
         nc.sync.dma_start(out=gates[:], in_=gate[:, 0:P, :].rearrange("r p t -> p r t"))
 
-        u_code, u_scale = [], []
-
-        def quantise_u(a):
-            grouped = held([P, T, PACK], BF16, "u_grouped%d" % a)
-            dst = grouped[:].rearrange("p (c i) j -> p c j i", i=4)
-            src = u_raw[a][:].rearrange("p j (c i) -> p c j i", i=4)
-            nc.vector.tensor_copy(out=dst[:, : U_SPLIT // 4], in_=src[:, : U_SPLIT // 4])
-            nc.scalar.copy(out=dst[:, U_SPLIT // 4 :], in_=src[:, U_SPLIT // 4 :])
-            codes = held([P, T], U32, "u_code%d" % a)
-            scales = held([P, T], U8, "u_scale%d" % a)
+        wu_code, wu_scale = [], []
+        for a in range(2):
+            grouped = held([P, PACK, P, PACK], BF16, "wu_grouped%d" % a)
+            dst = grouped[:].rearrange("p t m j -> p m t j")
+            src = wu_raw[a][:].rearrange("p j (m t) -> p m t j", t=PACK)
+            nc.vector.tensor_copy(out=dst[:, :M_SPLIT], in_=src[:, :M_SPLIT])
+            nc.scalar.copy(out=dst[:, M_SPLIT:], in_=src[:, M_SPLIT:])
+            wu_code.append(held([P, K], U32, "wu_code%d" % a))
+            wu_scale.append(held([P, K], U8, "wu_scale%d" % a))
             nc.vector.quantize_mx(
-                out=codes[:].bitcast(FP8X4), scales=scales[:], in_=grouped[:].rearrange("p t j -> p (t j)")
+                out=wu_code[a][:].bitcast(FP8X4),
+                scales=wu_scale[a][:],
+                in_=grouped[:].rearrange("p t m j -> p (t m j)"),
             )
-            u_code.append(codes)
-            u_scale.append(scales)
 
-        quantise_u(0)
+        u_grouped, u_quantised = {}, {}
 
-        wu_grouped0 = held([P, PACK, P, PACK], BF16, "wu_grouped0")
-        dst = wu_grouped0[:].rearrange("p t m j -> p m t j")
-        src = wu_raw0[:].rearrange("p j (m t) -> p m t j", t=PACK)
-        nc.vector.tensor_copy(out=dst[:, :M_SPLIT], in_=src[:, :M_SPLIT])
-        nc.scalar.copy(out=dst[:, M_SPLIT:], in_=src[:, M_SPLIT:])
-        wu_code0 = held([P, K], U32, "wu_code0")
-        wu_scale0 = held([P, K], U8, "wu_scale0")
-        nc.vector.quantize_mx(
-            out=wu_code0[:].bitcast(FP8X4), scales=wu_scale0[:], in_=wu_grouped0[:].rearrange("p t m j -> p (t m j)")
-        )
+        def round_u(load):
+            a, t0, t1, split = U_LOADS[load]
+            u_grouped[load] = held([P, t1 - t0, PACK], BF16, "u_grouped%d" % load)
+            dst = u_grouped[load][:].rearrange("p (c i) j -> p c j i", i=4)
+            src = u_raw[load][:].rearrange("p j (c i) -> p c j i", i=4)
+            nc.vector.tensor_copy(out=dst[:, : split // 4], in_=src[:, : split // 4])
+            if split < t1 - t0:
+                nc.scalar.copy(out=dst[:, split // 4 :], in_=src[:, split // 4 :])
+
+        def quantise_u(load):
+            a, t0, t1, split = U_LOADS[load]
+            codes = held([P, t1 - t0], U32, "u_code%d" % load)
+            scales = held([P, t1 - t0], U8, "u_scale%d" % load)
+            nc.vector.quantize_mx(
+                out=codes[:].bitcast(FP8X4), scales=scales[:], in_=u_grouped[load][:].rearrange("p t j -> p (t j)")
+            )
+            u_quantised[load] = (codes, scales)
 
         x_banks = {}
-        for t in range(PACK):
-            for h in range(2):
-                x_banks[t, h] = bank(4 * (t // 2) + 2 * h + t % 2)
-                nc.tensor.matmul_mx(
-                    out=x_banks[t, h][:, :HALF],
-                    lhsT=wu_code0[:, t * P : (t + 1) * P].bitcast(FP8X4),
-                    lhsT_scale=wu_scale0[:, t * P : (t + 1) * P],
-                    rhs=u_code[0][:, h * HALF : (h + 1) * HALF].bitcast(FP8X4),
-                    rhs_scale=u_scale[0][:, h * HALF : (h + 1) * HALF],
-                    start=True,
-                    stop=False,
-                )
 
-        quantise_u(1)
-
-        wu_grouped1 = [held([P, 2, P, PACK], BF16, "wu_grouped1_%d" % g) for g in range(2)]
-        for h in range(2):
-            src = wu_raw1[h][:].rearrange("p j (m t) -> p m t j", t=PACK)
-            for g in range(2):
-                dst = wu_grouped1[g][:].rearrange("p t m j -> p m t j")[:, :, :, 2 * h : 2 * h + 2]
-                if g == 0:
-                    nc.vector.tensor_copy(out=dst, in_=src[:, :, 0:2, :])
-                else:
-                    nc.scalar.copy(out=dst, in_=src[:, :, 2:4, :])
-        for g in range(2):
-            codes = held([P, 2 * P], U32, "wu_code1_%d" % g)
-            scales = held([P, 2 * P], U8, "wu_scale1_%d" % g)
-            nc.vector.quantize_mx(
-                out=codes[:].bitcast(FP8X4), scales=scales[:], in_=wu_grouped1[g][:].rearrange("p t m j -> p (t m j)")
+        def project(block, g, i, a):
+            t0, t1 = TOKEN_BLOCKS[block]
+            load = [n for n, (la, l0, l1, split) in enumerate(U_LOADS) if la == a and l0 <= t0 and t1 <= l1][0]
+            codes, scales = u_quantised[load]
+            tokens = slice(t0 - U_LOADS[load][1], t1 - U_LOADS[load][1])
+            if (block, g) not in x_banks:
+                x_banks[block, g] = bank(X_BANKS[2 * block + g])
+            cols = slice((2 * g + i) * P, (2 * g + i + 1) * P)
+            nc.tensor.matmul_mx(
+                out=x_banks[block, g][:, i * (t1 - t0) : (i + 1) * (t1 - t0)],
+                lhsT=wu_code[a][:, cols].bitcast(FP8X4),
+                lhsT_scale=wu_scale[a][:, cols],
+                rhs=codes[:, tokens].bitcast(FP8X4),
+                rhs_scale=scales[:, tokens],
+                start=(a == 0),
+                stop=(a == 1),
             )
-            pairs = x_pairs[g][:].bitcast(BF16).rearrange("p (w i) -> p w i", i=2)
-            for h in range(2):
-                for i in range(2):
-                    x_bank = x_banks[2 * g + i, h]
-                    nc.tensor.matmul_mx(
-                        out=x_bank[:, :HALF],
-                        lhsT=codes[:, i * P : (i + 1) * P].bitcast(FP8X4),
-                        lhsT_scale=scales[:, i * P : (i + 1) * P],
-                        rhs=u_code[1][:, h * HALF : (h + 1) * HALF].bitcast(FP8X4),
-                        rhs_scale=u_scale[1][:, h * HALF : (h + 1) * HALF],
-                        start=False,
-                        stop=True,
-                    )
-                    dst = pairs[:, h * HALF : (h + 1) * HALF, i]
-                    if g == 0 and h == 1:
-                        nc.vector.tensor_copy(out=dst, in_=x_bank[:, :HALF])
-                    else:
-                        nc.scalar.copy(out=dst, in_=x_bank[:, :HALF])
+
+        def open_block(block):
+            for g in range(2):
+                project(block, g, 0, 0)
+
+        def close_block(block):
+            t0, t1 = TOKEN_BLOCKS[block]
+            for g in range(2):
+                project(block, g, 0, 1)
+                project(block, g, 1, 0)
+                project(block, g, 1, 1)
+                dst = x_pairs[g][:, t0:t1].bitcast(BF16).rearrange("p (w i) -> p w i", i=2)
+                src = x_banks[block, g][:, : 2 * (t1 - t0)].rearrange("p (i w) -> p w i", i=2)
+                if block == len(TOKEN_BLOCKS) - 1 and g == 0:
+                    nc.vector.tensor_copy(out=dst, in_=src)
+                else:
+                    nc.scalar.copy(out=dst, in_=src)
+
+        for block in range(len(TOKEN_BLOCKS)):
+            round_u(2 * block)
+            round_u(2 * block + 1)
+            quantise_u(2 * block)
+            open_block(block)
+            quantise_u(2 * block + 1)
+            close_block(block)
 
         y = {0: held([P, S], F32, "y0")}
         slot_code, slot_scale, woven, gathered = {}, {}, {}, {}
@@ -299,14 +302,31 @@ def tile_moe_prv_lin_gelu_kernel(
         experts(2)
         turned = turned_sum(0, terms)
         terms = gated_terms(1)
-        accs = [products(e0, e1, 3) for e0, e1 in W_LOADS]
+        experts(3)
         turn_back_and_store(0, turned)
-        for (e0, e1), acc in zip(W_LOADS, accs):
-            gelus(e0, e1, 3, acc)
         turned = turned_sum(1, terms)
         terms = gated_terms(2)
         turn_back_and_store(1, turned)
-        turn_back_and_store(2, turned_sum(2, terms))
+        blocks = [slice(block * P, (block + 1) * P) for block in range(T // P)]
+        turned_blocks = [bank(block) for block in range(T // P)]
+        for r in range(TOP):
+            for cols, turned_block in zip(blocks, turned_blocks):
+                nc.tensor.matmul(
+                    out=turned_block[:, :P],
+                    lhsT=terms[r][:, cols],
+                    rhs=ident[:],
+                    is_transpose=True,
+                    start=(r == 0),
+                    stop=(r == TOP - 1),
+                )
+        back = bank(6)
+        for block, (cols, turned_block) in enumerate(zip(blocks, turned_blocks)):
+            staged_block = held([P, P], F32, "staged_block%d" % block)
+            nc.scalar.copy(out=staged_block[:], in_=turned_block[:, :P])
+            nc.tensor.transpose(back[:, cols], staged_block[:], ident[:])
+        result = ring.tile([P, T], F32, name="result", tag="result", align_bytes=64)
+        nc.scalar.copy(out=result[:], in_=back[:])
+        nc.sync.dma_start(out=out[2 * P : 3 * P, :], in_=result[:])
 
         last = N // P - 1
         last_terms = [held([P, T], F32, "last_term%d" % r) for r in range(TOP)]

@@ -25,13 +25,16 @@ PACK = 4
 HALF = T // 2
 WINDOW = 704
 TOKEN_BLOCKS = ((0, 128), (128, 256), (256, 384), (384, 512))
-U_LOADS = tuple((a, t0, t1, 80 if a == 0 or t1 == T else 128) for t0, t1 in TOKEN_BLOCKS for a in range(2))
+U_LOADS = ((0, 0, T, 320), (1, 0, 128, 0), (1, 128, 256, 0), (1, 256, 384, 0), (1, 384, 512, 128))
 X_BANKS = (0, 1, 2, 3, 4, 5, 6, 7)
-M_SPLIT = 80
+M_SPLIT = 88
 PIECES = ((0, 4), (4, 8), (8, 10), (10, 11), (11, 12))
 ORDER = "g0 g1 q0 g2 g3 q1 g4 q2 q3 q4"
 GATHER_TILES = (((0,), None), ((1,), None), ((2, 3), 0), ((4,), 1))
-LATER_BANKS = (0, 3, 2)
+LATER_BANKS = {1: (4, 5, 6), 2: (7, 0, 3), 3: (4, 5, 2)}
+TURN_BANKS = (6, 7, 3)
+BACK_BANKS = (1, 0, 1, 2)
+BLOCK_BANKS = (4, 5)
 W_LOADS = ((0, 4), (4, 8), (8, 12))
 
 
@@ -66,10 +69,10 @@ def tile_moe_prv_lin_gelu_kernel(
         u_rows = uT.rearrange("(a p j) t -> a p j t", p=P, j=PACK)
         wu_rows = wu.rearrange("(a p j) k -> a p j k", p=P, j=PACK)
         wu_raw = [held([P, PACK, K], F32, "wu_raw%d" % a) for a in range(2)]
-        for a in range(2):
-            nc.sync.dma_start(out=wu_raw[a][:], in_=wu_rows[a])
         u_raw = []
         for a, t0, t1, split in U_LOADS:
+            if t0 == 0:
+                nc.sync.dma_start(out=wu_raw[a][:], in_=wu_rows[a])
             raw = held([P, PACK, t1 - t0], F32, "u_raw%d_%d" % (a, t0))
             nc.sync.dma_start(out=raw[:], in_=u_rows[a][:, :, t0:t1])
             u_raw.append(raw)
@@ -100,20 +103,22 @@ def tile_moe_prv_lin_gelu_kernel(
         gates = held([P, TOP, T], F32, "gates")
         nc.sync.dma_start(out=gates[:], in_=gate[:, 0:P, :].rearrange("r p t -> p r t"))
 
-        wu_code, wu_scale = [], []
-        for a in range(2):
+        wu_code, wu_scale = {}, {}
+
+        def quantise_wu(a):
             grouped = held([P, PACK, P, PACK], BF16, "wu_grouped%d" % a)
             dst = grouped[:].rearrange("p t m j -> p m t j")
             src = wu_raw[a][:].rearrange("p j (m t) -> p m t j", t=PACK)
             nc.vector.tensor_copy(out=dst[:, :M_SPLIT], in_=src[:, :M_SPLIT])
             nc.scalar.copy(out=dst[:, M_SPLIT:], in_=src[:, M_SPLIT:])
-            wu_code.append(held([P, K], U32, "wu_code%d" % a))
-            wu_scale.append(held([P, K], U8, "wu_scale%d" % a))
-            nc.vector.quantize_mx(
-                out=wu_code[a][:].bitcast(FP8X4),
-                scales=wu_scale[a][:],
-                in_=grouped[:].rearrange("p t m j -> p (t m j)"),
-            )
+            for g in range(2):
+                wu_code[a, g] = held([P, 2 * P], U32, "wu_code%d_%d" % (a, g))
+                wu_scale[a, g] = held([P, 2 * P], U8, "wu_scale%d_%d" % (a, g))
+                nc.vector.quantize_mx(
+                    out=wu_code[a, g][:].bitcast(FP8X4),
+                    scales=wu_scale[a, g][:],
+                    in_=grouped[:, 2 * g : 2 * g + 2].rearrange("p t m j -> p (t m j)"),
+                )
 
         u_grouped, u_quantised = {}, {}
 
@@ -122,7 +127,8 @@ def tile_moe_prv_lin_gelu_kernel(
             u_grouped[load] = held([P, t1 - t0, PACK], BF16, "u_grouped%d" % load)
             dst = u_grouped[load][:].rearrange("p (c i) j -> p c j i", i=4)
             src = u_raw[load][:].rearrange("p j (c i) -> p c j i", i=4)
-            nc.vector.tensor_copy(out=dst[:, : split // 4], in_=src[:, : split // 4])
+            if split > 0:
+                nc.vector.tensor_copy(out=dst[:, : split // 4], in_=src[:, : split // 4])
             if split < t1 - t0:
                 nc.scalar.copy(out=dst[:, split // 4 :], in_=src[:, split // 4 :])
 
@@ -144,11 +150,11 @@ def tile_moe_prv_lin_gelu_kernel(
             tokens = slice(t0 - U_LOADS[load][1], t1 - U_LOADS[load][1])
             if (block, g) not in x_banks:
                 x_banks[block, g] = bank(X_BANKS[2 * block + g])
-            cols = slice((2 * g + i) * P, (2 * g + i + 1) * P)
+            cols = slice(i * P, (i + 1) * P)
             nc.tensor.matmul_mx(
                 out=x_banks[block, g][:, i * (t1 - t0) : (i + 1) * (t1 - t0)],
-                lhsT=wu_code[a][:, cols].bitcast(FP8X4),
-                lhsT_scale=wu_scale[a][:, cols],
+                lhsT=wu_code[a, g][:, cols].bitcast(FP8X4),
+                lhsT_scale=wu_scale[a, g][:, cols],
                 rhs=codes[:, tokens].bitcast(FP8X4),
                 rhs_scale=scales[:, tokens],
                 start=(a == 0),
@@ -167,17 +173,22 @@ def tile_moe_prv_lin_gelu_kernel(
                 project(block, g, 1, 1)
                 dst = x_pairs[g][:, t0:t1].bitcast(BF16).rearrange("p (w i) -> p w i", i=2)
                 src = x_banks[block, g][:, : 2 * (t1 - t0)].rearrange("p (i w) -> p w i", i=2)
-                if block == len(TOKEN_BLOCKS) - 1 and g == 0:
+                if block > 0 and g == 0:
                     nc.vector.tensor_copy(out=dst, in_=src)
                 else:
                     nc.scalar.copy(out=dst, in_=src)
 
+        quantise_wu(0)
+        round_u(0)
+        quantise_u(0)
         for block in range(len(TOKEN_BLOCKS)):
-            round_u(2 * block)
-            round_u(2 * block + 1)
-            quantise_u(2 * block)
             open_block(block)
-            quantise_u(2 * block + 1)
+        quantise_wu(1)
+        for block in range(len(TOKEN_BLOCKS)):
+            round_u(1 + block)
+        for block in range(len(TOKEN_BLOCKS)):
+            quantise_u(1 + block)
+        for block in range(len(TOKEN_BLOCKS)):
             close_block(block)
 
         y = {0: held([P, S], F32, "y0")}
@@ -216,7 +227,7 @@ def tile_moe_prv_lin_gelu_kernel(
         piece_of = {e: piece for piece, (e0, e1) in enumerate(PIECES) for e in range(e0, e1)}
 
         def products(e0, e1, j):
-            acc = bank(piece_of[e0] % 4 if j == 0 else LATER_BANKS[e0 // 4])
+            acc = bank(piece_of[e0] % 4 if j == 0 else LATER_BANKS[j][e0 // 4])
             for e in range(e0, e1):
                 piece = piece_of[e]
                 slots = slice((e - PIECES[piece][0]) * C, (e - PIECES[piece][0] + 1) * C)
@@ -272,7 +283,7 @@ def tile_moe_prv_lin_gelu_kernel(
             return terms
 
         def turned_sum(j, terms):
-            turned = bank(4 + j % 2)
+            turned = bank(TURN_BANKS[j])
             for block in range(T // P):
                 cols = slice(block * P, (block + 1) * P)
                 for r in range(TOP):
@@ -289,7 +300,7 @@ def tile_moe_prv_lin_gelu_kernel(
         def turn_back_and_store(j, turned):
             staged = ring.tile([P, T], F32, name="staged", tag="staged", align_bytes=64)
             nc.scalar.copy(out=staged[:], in_=turned[:])
-            back = bank(6 + j % 2)
+            back = bank(BACK_BANKS[j])
             for block in range(T // P):
                 cols = slice(block * P, (block + 1) * P)
                 nc.tensor.transpose(back[:, cols], staged[:, cols], ident[:])
@@ -297,47 +308,50 @@ def tile_moe_prv_lin_gelu_kernel(
             nc.scalar.copy(out=result[:], in_=back[:])
             nc.sync.dma_start(out=out[j * P : (j + 1) * P, :], in_=result[:])
 
-        experts(1)
-        terms = gated_terms(0)
-        experts(2)
-        turned = turned_sum(0, terms)
+        for j in range(1, N // P):
+            experts(j)
+        turned = turned_sum(0, gated_terms(0))
         terms = gated_terms(1)
-        experts(3)
         turn_back_and_store(0, turned)
         turned = turned_sum(1, terms)
         terms = gated_terms(2)
         turn_back_and_store(1, turned)
+        turn_back_and_store(2, turned_sum(2, terms))
+
+        last = N // P - 1
+        last_terms = [held([P, T], F32, "last_term%d" % r) for r in range(TOP)]
         blocks = [slice(block * P, (block + 1) * P) for block in range(T // P)]
-        turned_blocks = [bank(block) for block in range(T // P)]
+        turned_blocks = [bank(index) for index in BLOCK_BANKS]
         for r in range(TOP):
+            gated(last, r, slice(0, HALF), last_terms[r])
             for cols, turned_block in zip(blocks, turned_blocks):
                 nc.tensor.matmul(
                     out=turned_block[:, :P],
-                    lhsT=terms[r][:, cols],
+                    lhsT=last_terms[r][:, cols],
                     rhs=ident[:],
                     is_transpose=True,
                     start=(r == 0),
                     stop=(r == TOP - 1),
                 )
-        back = bank(6)
+        back = bank(BACK_BANKS[last])
         for block, (cols, turned_block) in enumerate(zip(blocks, turned_blocks)):
             staged_block = held([P, P], F32, "staged_block%d" % block)
             nc.scalar.copy(out=staged_block[:], in_=turned_block[:, :P])
             nc.tensor.transpose(back[:, cols], staged_block[:], ident[:])
-        result = ring.tile([P, T], F32, name="result", tag="result", align_bytes=64)
-        nc.scalar.copy(out=result[:], in_=back[:])
-        nc.sync.dma_start(out=out[2 * P : 3 * P, :], in_=result[:])
+        first_half = held([P, HALF], F32, "first_half")
+        nc.scalar.copy(out=first_half[:], in_=back[:, :HALF])
+        nc.sync.dma_start(out=out[last * P : (last + 1) * P, :HALF], in_=first_half[:])
 
-        last = N // P - 1
-        last_terms = [held([P, T], F32, "last_term%d" % r) for r in range(TOP)]
-        gated(last, 0, slice(0, T), last_terms[0])
-        gated(last, 1, slice(0, T), last_terms[1])
-        halves = [slice(0, HALF), slice(HALF, T)]
-        gated(last, 2, halves[0], last_terms[2])
-        partial = held([P, T], F32, "partial")
-        nc.vector.tensor_tensor(out=partial[:], in0=last_terms[0][:], in1=last_terms[1][:], op=ADD)
-        gated(last, 2, halves[1], last_terms[2])
-        for h, cols in enumerate(halves):
-            result = held([P, HALF], F32, "last_result%d" % h)
-            nc.vector.tensor_tensor(out=result[:], in0=partial[:, cols], in1=last_terms[2][:, cols], op=ADD)
-            nc.sync.dma_start(out=out[last * P : (last + 1) * P, cols], in_=result[:])
+        gated(last, 0, slice(HALF, T), last_terms[0])
+        gated(last, 1, slice(HALF, T), last_terms[1])
+        gated(last, 2, blocks[2], last_terms[2])
+        partial = held([P, HALF], F32, "partial")
+        nc.vector.tensor_tensor(out=partial[:], in0=last_terms[0][:, HALF:], in1=last_terms[1][:, HALF:], op=ADD)
+        gated(last, 2, blocks[3], last_terms[2])
+        second_half = held([P, HALF], F32, "second_half")
+        for block in (2, 3):
+            cols = slice((block - 2) * P, (block - 1) * P)
+            nc.vector.tensor_tensor(
+                out=second_half[:, cols], in0=partial[:, cols], in1=last_terms[2][:, blocks[block]], op=ADD
+            )
+        nc.sync.dma_start(out=out[last * P : (last + 1) * P, HALF:], in_=second_half[:])

from contextlib import ExitStack

import concourse.mybir as mybir
from concourse.masks import make_identity

F, K, T, E, C, N = 1024, 512, 512, 12, 128, 512
TOP = 3
S = E * C
FLOPS = 2 * F * K * T + 2 * K * N * S
BYTES = 4 * F * T + 4 * F * K + E * K * N + E * 16 * N + 4 * N * E + 4 * TOP * T + 2 * 128 * (S + TOP * T) // 16 + 4 * N * T

F32 = mybir.dt.float32
BF16 = mybir.dt.bfloat16
I32 = mybir.dt.int32
U32 = mybir.dt.uint32
U16 = mybir.dt.uint16
U8 = mybir.dt.uint8
FP8X4 = mybir.dt.float8_e4m3fn_x4
MULT = mybir.AluOpType.mult
ADD = mybir.AluOpType.add
GELU = mybir.ActivationFunctionType.Gelu_apprx_tanh

P = 128
PACK = 4
HALF = T // 2
WINDOW = 704
TOKEN_BLOCKS = ((0, 128), (128, 256), (256, 384), (384, 512))
U_LOADS = ((0, 0, T, 320), (1, 0, 128, 0), (1, 128, 256, 0), (1, 256, 384, 0), (1, 384, 512, 128))
X_BANKS = (0, 1, 2, 3, 4, 5, 6, 7)
M_SPLIT = 88
PIECES = ((0, 4), (4, 8), (8, 10), (10, 11), (11, 12))
ORDER = "g0 g1 q0 g2 g3 q1 g4 q2 q3 q4"
GATHER_TILES = (((0,), None), ((1,), None), ((2, 3), 0), ((4,), 1))
LATER_BANKS = {1: (4, 5, 6), 2: (7, 0, 3), 3: (4, 5, 2)}
TURN_BANKS = (6, 7, 3)
BACK_BANKS = (1, 0, 1, 2)
BLOCK_BANKS = (4, 5)
W_LOADS = ((0, 4), (4, 8), (8, 12))


def tile_moe_prv_lin_gelu_kernel(
    tc, uT, wu, w_words, w_scales, b, gate, offs, pos1, pos2, pos3, out
):
    nc = tc.nc
    with ExitStack() as ctx:
        keep = ctx.enter_context(tc.tile_pool(name="keep", bufs=1))
        ring = ctx.enter_context(tc.tile_pool(name="ring", bufs=2))
        psum = ctx.enter_context(tc.psum_pool(name="psum", bufs=1))

        def held(shape, dtype, name, tag=None):
            return keep.tile(shape, dtype, name=name, tag=tag or name, align_bytes=64)

        def bank(index):
            return psum.tile([P, 512], F32, name="bank%d" % index, tag="bank%d" % index)

        warm = held([P, 8], F32, "warm")
        nc.vector.memset(warm[:], 0.0)
        warm_out = held([P, 8], F32, "warm_out")
        nc.scalar.activation(out=warm_out[:], in_=warm[:], func=GELU)

        w_scale = held([P, E, N], U8, "w_scale")
        nc.gpsimd.memset(w_scale[:].bitcast(I32), 0)
        x_pairs = [held([P, WINDOW], U32, "x_pair%d" % h) for h in range(2)]
        for x_pair in x_pairs:
            nc.gpsimd.memset(x_pair[:, T:], 0)
        ident = held([P, P], F32, "ident")
        make_identity(nc, ident[:])

        u_rows = uT.rearrange("(a p j) t -> a p j t", p=P, j=PACK)
        wu_rows = wu.rearrange("(a p j) k -> a p j k", p=P, j=PACK)
        wu_raw = [held([P, PACK, K], F32, "wu_raw%d" % a) for a in range(2)]
        u_raw = []
        for a, t0, t1, split in U_LOADS:
            if t0 == 0:
                nc.sync.dma_start(out=wu_raw[a][:], in_=wu_rows[a])
            raw = held([P, PACK, t1 - t0], F32, "u_raw%d_%d" % (a, t0))
            nc.sync.dma_start(out=raw[:], in_=u_rows[a][:, :, t0:t1])
            u_raw.append(raw)
        slot_list = keep.tile([P, S // 16], U16, name="slot_list")
        nc.sync.dma_start(slot_list[:], offs)
        scale_rows = w_scales.rearrange("e a (q r) n -> r q (e a) n", r=4)
        for r in range(4):
            nc.sync.dma_start(out=w_scale[r:P:32, :, :].bitcast(I32), in_=scale_rows[r].bitcast(I32))
        bias = [held([P, E], F32, "bias%d" % j) for j in range(N // P)]
        w_code = {}
        for number, (e0, e1) in enumerate(W_LOADS):
            w_tile = held([P, e1 - e0, N], U32, "w_code%d" % e0)
            nc.sync.dma_start(
                out=w_tile[:].bitcast(I32),
                in_=w_words[e0:e1, 0].rearrange("e p n r -> p e (n r)").bitcast(I32),
            )
            for e in range(e0, e1):
                w_code[e] = w_tile[:, e - e0, :]
            if number == 0:
                nc.sync.dma_start(out=bias[0][:], in_=b[0:P, :])
        for j in range(1, N // P):
            nc.sync.dma_start(out=bias[j][:], in_=b[j * P : (j + 1) * P, :])
        pos_lists = []
        for r, pos in enumerate((pos1, pos2, pos3)):
            pos_list = keep.tile([P, T // 16], U16, name="pos_list%d" % r)
            nc.sync.dma_start(pos_list[:], pos)
            pos_lists.append(pos_list)
        gates = held([P, TOP, T], F32, "gates")
        nc.sync.dma_start(out=gates[:], in_=gate[:, 0:P, :].rearrange("r p t -> p r t"))

        wu_code, wu_scale = {}, {}

        def quantise_wu(a):
            grouped = held([P, PACK, P, PACK], BF16, "wu_grouped%d" % a)
            dst = grouped[:].rearrange("p t m j -> p m t j")
            src = wu_raw[a][:].rearrange("p j (m t) -> p m t j", t=PACK)
            nc.vector.tensor_copy(out=dst[:, :M_SPLIT], in_=src[:, :M_SPLIT])
            nc.scalar.copy(out=dst[:, M_SPLIT:], in_=src[:, M_SPLIT:])
            for g in range(2):
                wu_code[a, g] = held([P, 2 * P], U32, "wu_code%d_%d" % (a, g))
                wu_scale[a, g] = held([P, 2 * P], U8, "wu_scale%d_%d" % (a, g))
                nc.vector.quantize_mx(
                    out=wu_code[a, g][:].bitcast(FP8X4),
                    scales=wu_scale[a, g][:],
                    in_=grouped[:, 2 * g : 2 * g + 2].rearrange("p t m j -> p (t m j)"),
                )

        u_grouped, u_quantised = {}, {}

        def round_u(load):
            a, t0, t1, split = U_LOADS[load]
            u_grouped[load] = held([P, t1 - t0, PACK], BF16, "u_grouped%d" % load)
            dst = u_grouped[load][:].rearrange("p (c i) j -> p c j i", i=4)
            src = u_raw[load][:].rearrange("p j (c i) -> p c j i", i=4)
            if split > 0:
                nc.vector.tensor_copy(out=dst[:, : split // 4], in_=src[:, : split // 4])
            if split < t1 - t0:
                nc.scalar.copy(out=dst[:, split // 4 :], in_=src[:, split // 4 :])

        def quantise_u(load):
            a, t0, t1, split = U_LOADS[load]
            codes = held([P, t1 - t0], U32, "u_code%d" % load)
            scales = held([P, t1 - t0], U8, "u_scale%d" % load)
            nc.vector.quantize_mx(
                out=codes[:].bitcast(FP8X4), scales=scales[:], in_=u_grouped[load][:].rearrange("p t j -> p (t j)")
            )
            u_quantised[load] = (codes, scales)

        x_banks = {}

        def project(block, g, i, a):
            t0, t1 = TOKEN_BLOCKS[block]
            load = [n for n, (la, l0, l1, split) in enumerate(U_LOADS) if la == a and l0 <= t0 and t1 <= l1][0]
            codes, scales = u_quantised[load]
            tokens = slice(t0 - U_LOADS[load][1], t1 - U_LOADS[load][1])
            if (block, g) not in x_banks:
                x_banks[block, g] = bank(X_BANKS[2 * block + g])
            cols = slice(i * P, (i + 1) * P)
            nc.tensor.matmul_mx(
                out=x_banks[block, g][:, i * (t1 - t0) : (i + 1) * (t1 - t0)],
                lhsT=wu_code[a, g][:, cols].bitcast(FP8X4),
                lhsT_scale=wu_scale[a, g][:, cols],
                rhs=codes[:, tokens].bitcast(FP8X4),
                rhs_scale=scales[:, tokens],
                start=(a == 0),
                stop=(a == 1),
            )

        def open_block(block):
            for g in range(2):
                project(block, g, 0, 0)

        def close_block(block):
            t0, t1 = TOKEN_BLOCKS[block]
            for g in range(2):
                project(block, g, 0, 1)
                project(block, g, 1, 0)
                project(block, g, 1, 1)
                dst = x_pairs[g][:, t0:t1].bitcast(BF16).rearrange("p (w i) -> p w i", i=2)
                src = x_banks[block, g][:, : 2 * (t1 - t0)].rearrange("p (i w) -> p w i", i=2)
                if block > 0 and g == 0:
                    nc.vector.tensor_copy(out=dst, in_=src)
                else:
                    nc.scalar.copy(out=dst, in_=src)

        quantise_wu(0)
        round_u(0)
        quantise_u(0)
        for block in range(len(TOKEN_BLOCKS)):
            open_block(block)
        quantise_wu(1)
        for block in range(len(TOKEN_BLOCKS)):
            round_u(1 + block)
        for block in range(len(TOKEN_BLOCKS)):
            quantise_u(1 + block)
        for block in range(len(TOKEN_BLOCKS)):
            close_block(block)

        y = {0: held([P, S], F32, "y0")}
        slot_code, slot_scale, woven, gathered = {}, {}, {}, {}

        def gather_piece(piece):
            e0, e1 = PIECES[piece]
            width = (e1 - e0) * C
            for members, after in GATHER_TILES:
                if piece == members[0]:
                    total = sum((PIECES[m][1] - PIECES[m][0]) * C for m in members)
                    tile = held([P, 2 * total], U32, "gathered%d" % piece, None if after is None else "woven%d" % after)
                    start = 0
                    for m in members:
                        size = 2 * (PIECES[m][1] - PIECES[m][0]) * C
                        gathered[m] = tile[:, start : start + size].rearrange("p (g s) -> p g s", g=2)
                        start = start + size
            for g in range(2):
                nc.vector.tensor_copy(
                    out=gathered[piece][:, g, :], in_=x_pairs[g][:].indirect(slot_list[:, e0 * C // 16 : e1 * C // 16])
                )
            woven[piece] = held([P, width, 2], U32, "woven%d" % piece)
            nc.scalar.copy(out=woven[piece][:], in_=gathered[piece].rearrange("p g s -> p s g"))

        def quantise_piece(piece):
            e0, e1 = PIECES[piece]
            width = (e1 - e0) * C
            slot_code[piece] = held([P, width], U32, "slot_code%d" % piece)
            slot_scale[piece] = held([P, width], U8, "slot_scale%d" % piece)
            nc.vector.quantize_mx(
                out=slot_code[piece][:].bitcast(FP8X4),
                scales=slot_scale[piece][:],
                in_=woven[piece][:].rearrange("p s g -> p (s g)").bitcast(BF16),
            )

        piece_of = {e: piece for piece, (e0, e1) in enumerate(PIECES) for e in range(e0, e1)}

        def products(e0, e1, j):
            acc = bank(piece_of[e0] % 4 if j == 0 else LATER_BANKS[j][e0 // 4])
            for e in range(e0, e1):
                piece = piece_of[e]
                slots = slice((e - PIECES[piece][0]) * C, (e - PIECES[piece][0] + 1) * C)
                nc.tensor.matmul_mx(
                    out=acc[:, (e - e0) * C : (e - e0 + 1) * C],
                    lhsT=w_code[e][:, j * P : (j + 1) * P].bitcast(FP8X4),
                    lhsT_scale=w_scale[:, e, j * P : (j + 1) * P],
                    rhs=slot_code[piece][:, slots].bitcast(FP8X4),
                    rhs_scale=slot_scale[piece][:, slots],
                    start=True,
                    stop=True,
                )
            return acc

        def gelus(e0, e1, j, acc):
            if j not in y:
                y[j] = held([P, S], F32, "y%d" % j, "bias%d" % (j - 1))
            for e in range(e0, e1):
                nc.scalar.activation(
                    out=y[j][:, e * C : (e + 1) * C],
                    in_=acc[:, (e - e0) * C : (e - e0 + 1) * C],
                    func=GELU,
                    bias=bias[j][:, e : e + 1],
                )

        def experts(j):
            for e0, e1 in W_LOADS:
                gelus(e0, e1, j, products(e0, e1, j))

        for step in ORDER.split():
            piece = int(step[1:])
            if step[0] == "g":
                gather_piece(piece)
            else:
                quantise_piece(piece)
                e0, e1 = PIECES[piece]
                gelus(e0, e1, 0, products(e0, e1, 0))

        def gated(j, r, cols, term):
            nc.vector.tensor_tensor(
                out=term[:, cols],
                in0=y[j][:].indirect(pos_lists[r][:, cols.start // 16 : cols.stop // 16]),
                in1=gates[:, r, cols],
                op=MULT,
            )

        def gated_terms(j):
            terms = []
            for r in range(TOP):
                term = ring.tile([P, T], F32, name="term%d" % r, tag="term%d" % r, align_bytes=64)
                gated(j, r, slice(0, T), term)
                terms.append(term)
            return terms

        def turned_sum(j, terms):
            turned = bank(TURN_BANKS[j])
            for block in range(T // P):
                cols = slice(block * P, (block + 1) * P)
                for r in range(TOP):
                    nc.tensor.matmul(
                        out=turned[:, cols],
                        lhsT=terms[r][:, cols],
                        rhs=ident[:],
                        is_transpose=True,
                        start=(r == 0),
                        stop=(r == TOP - 1),
                    )
            return turned

        def turn_back_and_store(j, turned):
            staged = ring.tile([P, T], F32, name="staged", tag="staged", align_bytes=64)
            nc.scalar.copy(out=staged[:], in_=turned[:])
            back = bank(BACK_BANKS[j])
            for block in range(T // P):
                cols = slice(block * P, (block + 1) * P)
                nc.tensor.transpose(back[:, cols], staged[:, cols], ident[:])
            result = ring.tile([P, T], F32, name="result", tag="result", align_bytes=64)
            nc.scalar.copy(out=result[:], in_=back[:])
            nc.sync.dma_start(out=out[j * P : (j + 1) * P, :], in_=result[:])

        for j in range(1, N // P):
            experts(j)
        turned = turned_sum(0, gated_terms(0))
        terms = gated_terms(1)
        turn_back_and_store(0, turned)
        turned = turned_sum(1, terms)
        terms = gated_terms(2)
        turn_back_and_store(1, turned)
        turn_back_and_store(2, turned_sum(2, terms))

        last = N // P - 1
        last_terms = [held([P, T], F32, "last_term%d" % r) for r in range(TOP)]
        blocks = [slice(block * P, (block + 1) * P) for block in range(T // P)]
        turned_blocks = [bank(index) for index in BLOCK_BANKS]
        for r in range(TOP):
            gated(last, r, slice(0, HALF), last_terms[r])
            for cols, turned_block in zip(blocks, turned_blocks):
                nc.tensor.matmul(
                    out=turned_block[:, :P],
                    lhsT=last_terms[r][:, cols],
                    rhs=ident[:],
                    is_transpose=True,
                    start=(r == 0),
                    stop=(r == TOP - 1),
                )
        back = bank(BACK_BANKS[last])
        for block, (cols, turned_block) in enumerate(zip(blocks, turned_blocks)):
            staged_block = held([P, P], F32, "staged_block%d" % block)
            nc.scalar.copy(out=staged_block[:], in_=turned_block[:, :P])
            nc.tensor.transpose(back[:, cols], staged_block[:], ident[:])
        first_half = held([P, HALF], F32, "first_half")
        nc.scalar.copy(out=first_half[:], in_=back[:, :HALF])
        nc.sync.dma_start(out=out[last * P : (last + 1) * P, :HALF], in_=first_half[:])

        gated(last, 0, slice(HALF, T), last_terms[0])
        gated(last, 1, slice(HALF, T), last_terms[1])
        gated(last, 2, blocks[2], last_terms[2])
        partial = held([P, HALF], F32, "partial")
        nc.vector.tensor_tensor(out=partial[:], in0=last_terms[0][:, HALF:], in1=last_terms[1][:, HALF:], op=ADD)
        gated(last, 2, blocks[3], last_terms[2])
        second_half = held([P, HALF], F32, "second_half")
        for block in (2, 3):
            cols = slice((block - 2) * P, (block - 1) * P)
            nc.vector.tensor_tensor(
                out=second_half[:, cols], in0=partial[:, cols], in1=last_terms[2][:, blocks[block]], op=ADD
            )
        nc.sync.dma_start(out=out[last * P : (last + 1) * P, HALF:], in_=second_half[:])
